import numpy as np
import ml_dtypes


def mxq(x, axis, fmt="e4m3"):
    dtype, down = {"e4m3": (ml_dtypes.float8_e4m3fn, 7), "e5m2": (ml_dtypes.float8_e5m2, 14)}[fmt]
    v = np.moveaxis(np.asarray(x, np.float32).astype(ml_dtypes.bfloat16).astype(np.float64), axis, -1)
    blocks = v.reshape(v.shape[:-1] + (-1, 32))
    amax = np.abs(blocks).max(-1, keepdims=True)
    byte = np.maximum(np.where(amax > 0, np.frexp(amax)[1] - 1 + 127, 0) - down, 1)
    scale = np.exp2(byte - 127.0)
    codes = (blocks / scale).astype(np.float32).astype(dtype).astype(np.float64)
    return np.moveaxis((codes * scale).reshape(v.shape), -1, axis)


WIDE = False


def mx_kscale(k):
    if not WIDE:
        return np.ones(k)
    levels = np.array([10, -10, 5, -5, 0])
    if k % 512:
        return np.exp2(np.random.permutation(np.resize(levels, k // 32))).repeat(32)
    a = np.empty((k // 512, 16))
    for p in range(k // 512):
        a[p, :8] = np.random.permutation(np.resize(levels, 8))
        for g in range(8):
            far = levels[np.abs(levels - a[p, g]) >= 10]
            a[p, g + 8] = far[np.random.randint(len(far))]
    return np.exp2(a.ravel()).repeat(32)


def f64(x):
    return np.asarray(x).astype(np.float64)


def striped(idx):
    return np.tile(np.asarray(idx).reshape(-1, 16).T, (8, 1)).astype(np.uint16)


def unstriped(offs):
    return offs[:16].T.reshape(-1).astype(np.int64)


E2M1 = np.array([0.0, 0.5, 1.0, 1.5, 2.0, 3.0, 4.0, 6.0, -0.0, -0.5, -1.0, -1.5, -2.0, -3.0, -4.0, -6.0])


def pack_weight(w, fmt):
    k, n = w.shape
    w = f64(np.asarray(w, np.float32).astype(ml_dtypes.bfloat16)).reshape(k // 32, 32, n)
    amax = np.abs(w).max(1)
    if fmt == "e4m3":
        byte = np.frexp(amax)[1] - 1 + 127 - 7
    else:
        mant, ex = np.frexp(amax / 6.0)
        byte = np.where(mant > 0.5, ex, ex - 1) + 127
    byte = np.clip(np.where(amax > 0, byte, 1), 1, 254)
    scaled = (w * np.exp2(127.0 - byte)[:, None, :]).reshape(k, n).astype(np.float32)
    by_word = np.ascontiguousarray(scaled.reshape(k // 512, 128, 4, n).transpose(0, 1, 3, 2))
    if fmt == "e4m3":
        words = by_word.astype(ml_dtypes.float8_e4m3fn).view(np.uint8)
    else:
        c = by_word.astype(ml_dtypes.float4_e2m1fn).view(np.uint8) & 0xF
        words = (c[..., 0::2] | (c[..., 1::2] << 4)).reshape(k // 512, 128, 2 * n)
    return np.ascontiguousarray(words), np.ascontiguousarray(byte.astype(np.uint8).reshape(k // 512, 16, n))


def unpack_weight(words, scales, fmt):
    g, _, n = scales.shape
    words = np.ascontiguousarray(words).reshape(g, 128, n, -1)
    if fmt == "e4m3":
        vals = words.view(ml_dtypes.float8_e4m3fn).astype(np.float64)
    else:
        nib = np.empty((g, 128, n, 4), np.uint8)
        nib[..., 0::2] = words & 0xF
        nib[..., 1::2] = words >> 4
        vals = E2M1[nib]
    vals = vals * np.repeat(np.exp2(scales.astype(np.float64) - 127.0), 8, axis=1)[..., None]
    return vals.transpose(0, 1, 3, 2).reshape(g * 512, n)


def softplus(v):
    return np.log(1.0 + np.exp(v))


K, L, T, C, J = 1024, 512, 256, 1024, 512


def setup_inputs():
    n = np.random.standard_normal
    idx = np.random.permutation(C)[:J]
    fk = mx_kscale(K)
    fl = mx_kscale(L)
    wcp = pack_weight(n((K, C)) * 1 / np.sqrt(K) * fk[:, None], "e2m1")
    xsp = pack_weight(n((L, T)) / fl[:, None], "e4m3")
    wsp = pack_weight(n((L, J)) * 1 / np.sqrt(L) * fl[:, None], "e2m1")
    return {
        "xt": (n((K, T)) / fk[:, None]).astype(np.float32),
        "wc_words": wcp[0],
        "wc_scales": wcp[1],
        "sh": (np.random.uniform(0.01, 0.05, (1, J))).astype(np.float32),
        "xs_words": xsp[0],
        "xs_scales": xsp[1],
        "ws_words": wsp[0],
        "ws_scales": wsp[1],
        "offs": striped(idx),
    }


def reference(xt, wc_words, wc_scales, sh, xs_words, xs_scales, ws_words, ws_scales, offs):
    idx = unstriped(offs)
    wcu = unpack_weight(wc_words, wc_scales, "e2m1")
    xsu = unpack_weight(xs_words, xs_scales, "e4m3")
    wsu = unpack_weight(ws_words, ws_scales, "e2m1")
    xtq = mxq(f64(xt), 0, "e4m3")
    z = xtq.T @ wcu
    s = xsu.T @ wsu
    y = softplus(z[:, idx] + f64(sh) * np.sum(z, axis=1, keepdims=True)) - 0.5 * s
    return y

@@ -1,0 +1,181 @@
+import math
+from contextlib import ExitStack
+
+import concourse.mybir as mybir
+from concourse.masks import make_identity
+
+K, L, T, C, J = 1024, 512, 256, 1024, 512
+FLOPS = 2 * T * (K * C + L * J)
+
+F32 = mybir.dt.float32
+BF16 = mybir.dt.bfloat16
+I32 = mybir.dt.int32
+U32 = mybir.dt.uint32
+U16 = mybir.dt.uint16
+U8 = mybir.dt.uint8
+E4M3X4 = mybir.dt.float8_e4m3fn_x4
+E2M1X4 = mybir.dt.float4_e2m1fn_x4
+ALU = mybir.AluOpType
+ACT = mybir.ActivationFunctionType
+
+P = 128
+PACK = 4
+K_PASS = P * PACK
+PASSES = K // K_PASS
+TILES = T // P
+BANK = 512
+BANKS = C // BANK
+HALF = J // 2
+KNEE = 32.0
+
+
+def load_scale_rows(queue, plane, rows):
+    for quad in range(4):
+        queue.dma_start(
+            out=plane[32 * quad : 32 * quad + 4].bitcast(I32),
+            in_=rows[:, 4 * quad : 4 * quad + 4, :].rearrange("z r n -> r z n").bitcast(I32),
+        )
+
+
+def tile_list_kept_features_and_row_sum_kernel(
+    tc, xt, wc_words, wc_scales, sh, xs_words, xs_scales, ws_words, ws_scales, offs, out
+):
+    nc = tc.nc
+    with ExitStack() as ctx:
+        keep = ctx.enter_context(tc.tile_pool(name="keep", bufs=1))
+        psum = ctx.enter_context(tc.psum_pool(name="psum", bufs=1))
+
+        offsets = keep.tile([P, J // 16], U16, name="offsets")
+        wc_plane = keep.tile([P, PASSES, C], U8, name="wc_plane", align_bytes=64)
+        xs_plane = keep.tile([P, 1, T], U8, name="xs_plane", align_bytes=64)
+        ws_plane = keep.tile([P, 1, J], U8, name="ws_plane", align_bytes=64)
+        for plane in (wc_plane, xs_plane, ws_plane):
+            nc.vector.memset(plane[:].bitcast(I32), 0)
+
+        sh_rows = keep.tile([P, PACK], F32, name="sh_rows")
+        nc.gpsimd.dma_start(out=sh_rows[:], in_=sh.rearrange("o (p i) -> (o p) i", i=PACK))
+        ident = keep.tile([P, P], F32, name="ident")
+        make_identity(nc, ident[:])
+
+        x_raw = [keep.tile([P, PACK, T], F32, name=f"x_raw{a}") for a in range(PASSES)]
+        wc_codes = [keep.tile([P, 2 * C], U8, name=f"wc_codes{a}", align_bytes=64) for a in range(PASSES)]
+        for a in range(PASSES):
+            nc.sync.dma_start(
+                out=x_raw[a][:],
+                in_=xt[a * K_PASS : (a + 1) * K_PASS, :].rearrange("(p i) t -> p i t", i=PACK),
+            )
+            if a == 0:
+                load_scale_rows(nc.sync, wc_plane, wc_scales)
+            nc.sync.dma_start(out=wc_codes[a][:].bitcast(I32), in_=wc_words[a].bitcast(I32))
+        nc.sync.dma_start(offsets[:], offs)
+        xs_codes = keep.tile([P, PACK * T], U8, name="xs_codes", align_bytes=64)
+        ws_codes = keep.tile([P, 2 * J], U8, name="ws_codes", align_bytes=64)
+        nc.sync.dma_start(
+            out=xs_codes[:].bitcast(I32), in_=xs_words[0].rearrange("p t r -> p (t r)").bitcast(I32)
+        )
+        nc.sync.dma_start(out=ws_codes[:].bitcast(I32), in_=ws_words[0].bitcast(I32))
+        load_scale_rows(nc.sync, ws_plane, ws_scales)
+        load_scale_rows(nc.gpsimd, xs_plane, xs_scales)
+
+        sh_bank = psum.tile([P, PACK, P], F32, name="sh_bank")
+        for i in range(PACK):
+            nc.tensor.transpose(sh_bank[:, i, :], sh_rows[:, i : i + 1].to_broadcast([P, P]), ident[:])
+
+        z_bank = [[psum.tile([P, BANK], F32, name=f"z_bank{m}{b}") for b in range(BANKS)] for m in range(TILES)]
+        x_mx = {}
+        for a in range(PASSES):
+            grouped = []
+            for m in range(TILES):
+                g = keep.tile([P, P, PACK], BF16, name=f"grouped{a}{m}", align_bytes=64)
+                nc.vector.tensor_copy(
+                    out=g[:].rearrange("p (c u) i -> p c i u", u=4),
+                    in_=x_raw[a][:, :, m * P : (m + 1) * P].rearrange("p i (c u) -> p c i u", u=4),
+                )
+                grouped.append(g)
+            for m in range(TILES):
+                x_codes = keep.tile([P, P], U32, name=f"x_codes{a}{m}", align_bytes=64)
+                x_plane = keep.tile([P, P], U8, name=f"x_plane{a}{m}", align_bytes=64)
+                nc.vector.quantize_mx(
+                    out=x_codes[:].bitcast(E4M3X4),
+                    scales=x_plane[:],
+                    in_=grouped[m][:].rearrange("p t i -> p (t i)"),
+                )
+                x_mx[a, m] = (x_codes, x_plane)
+        for m in range(TILES):
+            for a in range(PASSES):
+                x_codes, x_plane = x_mx[a, m]
+                for b in range(BANKS):
+                    nc.tensor.matmul_mx(
+                        out=z_bank[m][b][:],
+                        lhsT=x_codes[:].bitcast(E4M3X4),
+                        lhsT_scale=x_plane[:],
+                        rhs=wc_codes[a][:, 2 * BANK * b : 2 * BANK * (b + 1)].bitcast(E2M1X4),
+                        rhs_scale=wc_plane[:, a, BANK * b : BANK * (b + 1)],
+                        start=(a == 0),
+                        stop=(a == PASSES - 1),
+                    )
+
+        s_bank = [psum.tile([P, J], F32, name=f"s_bank{m}") for m in range(TILES)]
+        for m in range(TILES):
+            nc.tensor.matmul_mx(
+                out=s_bank[m][:],
+                lhsT=xs_codes[:, PACK * P * m : PACK * P * (m + 1)].bitcast(E4M3X4),
+                lhsT_scale=xs_plane[:, 0, P * m : P * (m + 1)],
+                rhs=ws_codes[:].bitcast(E2M1X4),
+                rhs_scale=ws_plane[:, 0, :],
+                start=True,
+                stop=True,
+            )
+
+        v = keep.tile([P, TILES * J], F32, name="v")
+        e = keep.tile([P, TILES * J], F32, name="e")
+        for m in range(TILES):
+            z = keep.tile([P, C], F32, name=f"z{m}")
+            sum0 = keep.tile([P, 1], F32, name=f"sum0_{m}")
+            sum1 = keep.tile([P, 1], F32, name=f"sum1_{m}")
+            row_sum = keep.tile([P, 1], F32, name=f"row_sum{m}")
+            nc.scalar.activation(out=z[:, :BANK], in_=z_bank[m][0][:], func=ACT.Copy, accum_out=sum0[:])
+            nc.vector.tensor_scalar(
+                out=z[:, BANK:], in0=z_bank[m][1][:], scalar1=1.0, scalar2=None,
+                op0=ALU.mult, op1=ALU.add, accum_out=sum1[:],
+            )
+            nc.vector.tensor_tensor(out=row_sum[:], in0=sum0[:], in1=sum1[:], op=ALU.add)
+            picked = [keep.tile([P, HALF], F32, name=f"picked{m}{h}") for h in range(2)]
+            nc.vector.tensor_copy(out=picked[0][:], in_=z[:].indirect(offsets[:, : HALF // 16]))
+            nc.scalar.activation(out=picked[1][:], in_=z[:].indirect(offsets[:, HALF // 16 :]), func=ACT.Copy)
+            for h in range(2):
+                cols = slice(m * J + h * HALF, m * J + (h + 1) * HALF)
+                rows = slice(h * HALF // PACK, (h + 1) * HALF // PACK)
+                nc.vector.scalar_tensor_tensor(
+                    out=v[:, cols].rearrange("p (q i) -> p q i", i=PACK),
+                    in0=sh_bank[:, :, rows].rearrange("p i q -> p q i"),
+                    scalar=row_sum[:],
+                    in1=picked[h][:].rearrange("p (q i) -> p q i", i=PACK),
+                    op0=ALU.mult,
+                    op1=ALU.add,
+                )
+                nc.scalar.activation(out=e[:, cols], in_=v[:, cols], func=ACT.Exp)
+
+        capped = keep.tile([P, TILES * J], F32, name="capped")
+        nc.vector.tensor_scalar(
+            out=capped[:], in0=e[:], scalar1=math.exp(KNEE), scalar2=None, op0=ALU.min
+        )
+        above = keep.tile([P, TILES * J], F32, name="above")
+        rest = keep.tile([P, TILES * J], F32, name="rest")
+        for m in range(TILES):
+            cols = slice(m * J, (m + 1) * J)
+            nc.vector.tensor_scalar(
+                out=above[:, cols], in0=v[:, cols], scalar1=-KNEE, scalar2=0.0, op0=ALU.add, op1=ALU.max
+            )
+            nc.vector.scalar_tensor_tensor(
+                out=rest[:, cols], in0=s_bank[m][:], scalar=-0.5, in1=above[:, cols],
+                op0=ALU.mult, op1=ALU.add,
+            )
+        for m in range(TILES):
+            for h in range(2):
+                cols = slice(m * J + h * HALF, m * J + (h + 1) * HALF)
+                soft = keep.tile([P, HALF], F32, name=f"soft{m}{h}")
+                y = keep.tile([P, HALF], F32, name=f"y{m}{h}")
+                nc.scalar.activation(out=soft[:], in_=capped[:, cols], func=ACT.Ln, bias=1.0)
+                nc.vector.tensor_tensor(out=y[:], in0=soft[:], in1=rest[:, cols], op=ALU.add)
+                nc.sync.dma_start(out=out[m * P : (m + 1) * P, h * HALF : (h + 1) * HALF], in_=y[:])

@@ -2,7 +2,6 @@ import math
 from contextlib import ExitStack
 
 import concourse.mybir as mybir
-from concourse.masks import make_identity
 
 K, L, T, C, J = 1024, 512, 256, 1024, 512
 FLOPS = 2 * T * (K * C + L * J)
@@ -53,9 +52,20 @@ def tile_list_kept_features_and_row_sum_kernel(
             nc.vector.memset(plane[:].bitcast(I32), 0)
 
         sh_rows = keep.tile([P, PACK], F32, name="sh_rows")
-        nc.gpsimd.dma_start(out=sh_rows[:], in_=sh.rearrange("o (p i) -> (o p) i", i=PACK))
+        nc.sync.dma_start(out=sh_rows[:], in_=sh.rearrange("o (p i) -> (o p) i", i=PACK))
         ident = keep.tile([P, P], F32, name="ident")
-        make_identity(nc, ident[:])
+        ones = keep.tile([P, 32], F32, name="ones")
+        column = keep.tile([P, 32], F32, name="column", align_bytes=64)
+        row = keep.tile([P, 32], F32, name="row", align_bytes=64)
+        nc.vector.memset(ones[:], 1.0)
+        nc.vector.memset(ident[:], 0.0)
+        nc.vector.tensor_tensor_scan(
+            out=column[:], data0=ones[:], data1=ones[:], initial=0.0, op0=ALU.mult, op1=ALU.add
+        )
+        nc.vector.transpose(out=row[:], in_=column[:])
+        for quad in range(4):
+            part = slice(32 * quad, 32 * (quad + 1))
+            nc.vector.tensor_tensor(out=ident[part, part], in0=column[part, :], in1=row[part, :], op=ALU.is_equal)
 
         x_raw = [keep.tile([P, PACK, T], F32, name=f"x_raw{a}") for a in range(PASSES)]
         wc_codes = [keep.tile([P, 2 * C], U8, name=f"wc_codes{a}", align_bytes=64) for a in range(PASSES)]
@@ -75,7 +85,7 @@ def tile_list_kept_features_and_row_sum_kernel(
         )
         nc.sync.dma_start(out=ws_codes[:].bitcast(I32), in_=ws_words[0].bitcast(I32))
         load_scale_rows(nc.sync, ws_plane, ws_scales)
-        load_scale_rows(nc.gpsimd, xs_plane, xs_scales)
+        load_scale_rows(nc.sync, xs_plane, xs_scales)
 
         sh_bank = psum.tile([P, PACK, P], F32, name="sh_bank")
         for i in range(PACK):
@@ -139,10 +149,10 @@ def tile_list_kept_features_and_row_sum_kernel(
                 out=z[:, BANK:], in0=z_bank[m][1][:], scalar1=1.0, scalar2=None,
                 op0=ALU.mult, op1=ALU.add, accum_out=sum1[:],
             )
-            nc.vector.tensor_tensor(out=row_sum[:], in0=sum0[:], in1=sum1[:], op=ALU.add)
+            nc.scalar.activation(out=row_sum[:], in_=sum1[:], func=ACT.Identity, bias=sum0[:])
             picked = [keep.tile([P, HALF], F32, name=f"picked{m}{h}") for h in range(2)]
-            nc.vector.tensor_copy(out=picked[0][:], in_=z[:].indirect(offsets[:, : HALF // 16]))
-            nc.scalar.activation(out=picked[1][:], in_=z[:].indirect(offsets[:, HALF // 16 :]), func=ACT.Copy)
+            nc.scalar.activation(out=picked[0][:], in_=z[:].indirect(offsets[:, : HALF // 16]), func=ACT.Copy)
+            nc.vector.tensor_copy(out=picked[1][:], in_=z[:].indirect(offsets[:, HALF // 16 :]))
             for h in range(2):
                 cols = slice(m * J + h * HALF, m * J + (h + 1) * HALF)
                 rows = slice(h * HALF // PACK, (h + 1) * HALF // PACK)
@@ -156,17 +166,17 @@ def tile_list_kept_features_and_row_sum_kernel(
                 )
                 nc.scalar.activation(out=e[:, cols], in_=v[:, cols], func=ACT.Exp)
 
+        above = keep.tile([P, TILES * J], F32, name="above")
+        nc.vector.tensor_scalar(
+            out=above[:], in0=v[:], scalar1=-KNEE, scalar2=0.0, op0=ALU.add, op1=ALU.max
+        )
         capped = keep.tile([P, TILES * J], F32, name="capped")
         nc.vector.tensor_scalar(
             out=capped[:], in0=e[:], scalar1=math.exp(KNEE), scalar2=None, op0=ALU.min
         )
-        above = keep.tile([P, TILES * J], F32, name="above")
         rest = keep.tile([P, TILES * J], F32, name="rest")
         for m in range(TILES):
             cols = slice(m * J, (m + 1) * J)
-            nc.vector.tensor_scalar(
-                out=above[:, cols], in0=v[:, cols], scalar1=-KNEE, scalar2=0.0, op0=ALU.add, op1=ALU.max
-            )
             nc.vector.scalar_tensor_tensor(
                 out=rest[:, cols], in0=s_bank[m][:], scalar=-0.5, in1=above[:, cols],
                 op0=ALU.mult, op1=ALU.add,

@@ -52,7 +52,6 @@ def tile_list_kept_features_and_row_sum_kernel(
             nc.vector.memset(plane[:].bitcast(I32), 0)
 
         sh_rows = keep.tile([P, PACK], F32, name="sh_rows")
-        nc.sync.dma_start(out=sh_rows[:], in_=sh.rearrange("o (p i) -> (o p) i", i=PACK))
         ident = keep.tile([P, P], F32, name="ident")
         ones = keep.tile([P, 32], F32, name="ones")
         column = keep.tile([P, 32], F32, name="column", align_bytes=64)
@@ -78,6 +77,7 @@ def tile_list_kept_features_and_row_sum_kernel(
                 load_scale_rows(nc.sync, wc_plane, wc_scales)
             nc.sync.dma_start(out=wc_codes[a][:].bitcast(I32), in_=wc_words[a].bitcast(I32))
         nc.sync.dma_start(offsets[:], offs)
+        nc.sync.dma_start(out=sh_rows[:], in_=sh.rearrange("o (p i) -> (o p) i", i=PACK))
         xs_codes = keep.tile([P, PACK * T], U8, name="xs_codes", align_bytes=64)
         ws_codes = keep.tile([P, 2 * J], U8, name="ws_codes", align_bytes=64)
         nc.sync.dma_start(
@@ -87,17 +87,14 @@ def tile_list_kept_features_and_row_sum_kernel(
         load_scale_rows(nc.sync, ws_plane, ws_scales)
         load_scale_rows(nc.sync, xs_plane, xs_scales)
 
-        sh_bank = psum.tile([P, PACK, P], F32, name="sh_bank")
-        for i in range(PACK):
-            nc.tensor.transpose(sh_bank[:, i, :], sh_rows[:, i : i + 1].to_broadcast([P, P]), ident[:])
-
         z_bank = [[psum.tile([P, BANK], F32, name=f"z_bank{m}{b}") for b in range(BANKS)] for m in range(TILES)]
         x_mx = {}
         for a in range(PASSES):
             grouped = []
             for m in range(TILES):
                 g = keep.tile([P, P, PACK], BF16, name=f"grouped{a}{m}", align_bytes=64)
-                nc.vector.tensor_copy(
+                cast = nc.vector.tensor_copy if m == 0 else nc.scalar.copy
+                cast(
                     out=g[:].rearrange("p (c u) i -> p c i u", u=4),
                     in_=x_raw[a][:, :, m * P : (m + 1) * P].rearrange("p i (c u) -> p c i u", u=4),
                 )
@@ -124,6 +121,10 @@ def tile_list_kept_features_and_row_sum_kernel(
                         start=(a == 0),
                         stop=(a == PASSES - 1),
                     )
+
+        sh_bank = psum.tile([P, PACK, P], F32, name="sh_bank")
+        for i in range(PACK):
+            nc.tensor.transpose(sh_bank[:, i, :], sh_rows[:, i : i + 1].to_broadcast([P, P]), ident[:])
 
         s_bank = [psum.tile([P, J], F32, name=f"s_bank{m}") for m in range(TILES)]
         for m in range(TILES):

import math
from contextlib import ExitStack

import concourse.mybir as mybir

K, L, T, C, J = 1024, 512, 256, 1024, 512
FLOPS = 2 * T * (K * C + L * J)

F32 = mybir.dt.float32
BF16 = mybir.dt.bfloat16
I32 = mybir.dt.int32
U32 = mybir.dt.uint32
U16 = mybir.dt.uint16
U8 = mybir.dt.uint8
E4M3X4 = mybir.dt.float8_e4m3fn_x4
E2M1X4 = mybir.dt.float4_e2m1fn_x4
ALU = mybir.AluOpType
ACT = mybir.ActivationFunctionType

P = 128
PACK = 4
K_PASS = P * PACK
PASSES = K // K_PASS
TILES = T // P
BANK = 512
BANKS = C // BANK
HALF = J // 2
KNEE = 32.0


def load_scale_rows(queue, plane, rows):
    for quad in range(4):
        queue.dma_start(
            out=plane[32 * quad : 32 * quad + 4].bitcast(I32),
            in_=rows[:, 4 * quad : 4 * quad + 4, :].rearrange("z r n -> r z n").bitcast(I32),
        )


def tile_list_kept_features_and_row_sum_kernel(
    tc, xt, wc_words, wc_scales, sh, xs_words, xs_scales, ws_words, ws_scales, offs, out
):
    nc = tc.nc
    with ExitStack() as ctx:
        keep = ctx.enter_context(tc.tile_pool(name="keep", bufs=1))
        psum = ctx.enter_context(tc.psum_pool(name="psum", bufs=1))

        offsets = keep.tile([P, J // 16], U16, name="offsets")
        wc_plane = keep.tile([P, PASSES, C], U8, name="wc_plane", align_bytes=64)
        xs_plane = keep.tile([P, 1, T], U8, name="xs_plane", align_bytes=64)
        ws_plane = keep.tile([P, 1, J], U8, name="ws_plane", align_bytes=64)
        for plane in (wc_plane, xs_plane, ws_plane):
            nc.vector.memset(plane[:].bitcast(I32), 0)

        sh_rows = keep.tile([P, PACK], F32, name="sh_rows")
        ident = keep.tile([P, P], F32, name="ident")
        ones = keep.tile([P, 32], F32, name="ones")
        column = keep.tile([P, 32], F32, name="column", align_bytes=64)
        row = keep.tile([P, 32], F32, name="row", align_bytes=64)
        nc.vector.memset(ones[:], 1.0)
        nc.vector.memset(ident[:], 0.0)
        nc.vector.tensor_tensor_scan(
            out=column[:], data0=ones[:], data1=ones[:], initial=0.0, op0=ALU.mult, op1=ALU.add
        )
        nc.vector.transpose(out=row[:], in_=column[:])
        for quad in range(4):
            part = slice(32 * quad, 32 * (quad + 1))
            nc.vector.tensor_tensor(out=ident[part, part], in0=column[part, :], in1=row[part, :], op=ALU.is_equal)

        x_raw = [keep.tile([P, PACK, T], F32, name=f"x_raw{a}") for a in range(PASSES)]
        wc_codes = [keep.tile([P, 2 * C], U8, name=f"wc_codes{a}", align_bytes=64) for a in range(PASSES)]
        for a in range(PASSES):
            nc.sync.dma_start(
                out=x_raw[a][:],
                in_=xt[a * K_PASS : (a + 1) * K_PASS, :].rearrange("(p i) t -> p i t", i=PACK),
            )
            if a == 0:
                load_scale_rows(nc.sync, wc_plane, wc_scales)
            nc.sync.dma_start(out=wc_codes[a][:].bitcast(I32), in_=wc_words[a].bitcast(I32))
        nc.sync.dma_start(offsets[:], offs)
        nc.sync.dma_start(out=sh_rows[:], in_=sh.rearrange("o (p i) -> (o p) i", i=PACK))
        xs_codes = keep.tile([P, PACK * T], U8, name="xs_codes", align_bytes=64)
        ws_codes = keep.tile([P, 2 * J], U8, name="ws_codes", align_bytes=64)
        nc.sync.dma_start(
            out=xs_codes[:].bitcast(I32), in_=xs_words[0].rearrange("p t r -> p (t r)").bitcast(I32)
        )
        nc.sync.dma_start(out=ws_codes[:].bitcast(I32), in_=ws_words[0].bitcast(I32))
        load_scale_rows(nc.sync, ws_plane, ws_scales)
        load_scale_rows(nc.sync, xs_plane, xs_scales)

        z_bank = [[psum.tile([P, BANK], F32, name=f"z_bank{m}{b}") for b in range(BANKS)] for m in range(TILES)]
        x_mx = {}
        for a in range(PASSES):
            grouped = []
            for m in range(TILES):
                g = keep.tile([P, P, PACK], BF16, name=f"grouped{a}{m}", align_bytes=64)
                cast = nc.vector.tensor_copy if m == 0 else nc.scalar.copy
                cast(
                    out=g[:].rearrange("p (c u) i -> p c i u", u=4),
                    in_=x_raw[a][:, :, m * P : (m + 1) * P].rearrange("p i (c u) -> p c i u", u=4),
                )
                grouped.append(g)
            for m in range(TILES):
                x_codes = keep.tile([P, P], U32, name=f"x_codes{a}{m}", align_bytes=64)
                x_plane = keep.tile([P, P], U8, name=f"x_plane{a}{m}", align_bytes=64)
                nc.vector.quantize_mx(
                    out=x_codes[:].bitcast(E4M3X4),
                    scales=x_plane[:],
                    in_=grouped[m][:].rearrange("p t i -> p (t i)"),
                )
                x_mx[a, m] = (x_codes, x_plane)
        for m in range(TILES):
            for a in range(PASSES):
                x_codes, x_plane = x_mx[a, m]
                for b in range(BANKS):
                    nc.tensor.matmul_mx(
                        out=z_bank[m][b][:],
                        lhsT=x_codes[:].bitcast(E4M3X4),
                        lhsT_scale=x_plane[:],
                        rhs=wc_codes[a][:, 2 * BANK * b : 2 * BANK * (b + 1)].bitcast(E2M1X4),
                        rhs_scale=wc_plane[:, a, BANK * b : BANK * (b + 1)],
                        start=(a == 0),
                        stop=(a == PASSES - 1),
                    )

        sh_bank = psum.tile([P, PACK, P], F32, name="sh_bank")
        for i in range(PACK):
            nc.tensor.transpose(sh_bank[:, i, :], sh_rows[:, i : i + 1].to_broadcast([P, P]), ident[:])

        s_bank = [psum.tile([P, J], F32, name=f"s_bank{m}") for m in range(TILES)]
        for m in range(TILES):
            nc.tensor.matmul_mx(
                out=s_bank[m][:],
                lhsT=xs_codes[:, PACK * P * m : PACK * P * (m + 1)].bitcast(E4M3X4),
                lhsT_scale=xs_plane[:, 0, P * m : P * (m + 1)],
                rhs=ws_codes[:].bitcast(E2M1X4),
                rhs_scale=ws_plane[:, 0, :],
                start=True,
                stop=True,
            )

        v = keep.tile([P, TILES * J], F32, name="v")
        e = keep.tile([P, TILES * J], F32, name="e")
        for m in range(TILES):
            z = keep.tile([P, C], F32, name=f"z{m}")
            sum0 = keep.tile([P, 1], F32, name=f"sum0_{m}")
            sum1 = keep.tile([P, 1], F32, name=f"sum1_{m}")
            row_sum = keep.tile([P, 1], F32, name=f"row_sum{m}")
            nc.scalar.activation(out=z[:, :BANK], in_=z_bank[m][0][:], func=ACT.Copy, accum_out=sum0[:])
            nc.vector.tensor_scalar(
                out=z[:, BANK:], in0=z_bank[m][1][:], scalar1=1.0, scalar2=None,
                op0=ALU.mult, op1=ALU.add, accum_out=sum1[:],
            )
            nc.scalar.activation(out=row_sum[:], in_=sum1[:], func=ACT.Identity, bias=sum0[:])
            picked = [keep.tile([P, HALF], F32, name=f"picked{m}{h}") for h in range(2)]
            nc.scalar.activation(out=picked[0][:], in_=z[:].indirect(offsets[:, : HALF // 16]), func=ACT.Copy)
            nc.vector.tensor_copy(out=picked[1][:], in_=z[:].indirect(offsets[:, HALF // 16 :]))
            for h in range(2):
                cols = slice(m * J + h * HALF, m * J + (h + 1) * HALF)
                rows = slice(h * HALF // PACK, (h + 1) * HALF // PACK)
                nc.vector.scalar_tensor_tensor(
                    out=v[:, cols].rearrange("p (q i) -> p q i", i=PACK),
                    in0=sh_bank[:, :, rows].rearrange("p i q -> p q i"),
                    scalar=row_sum[:],
                    in1=picked[h][:].rearrange("p (q i) -> p q i", i=PACK),
                    op0=ALU.mult,
                    op1=ALU.add,
                )
                nc.scalar.activation(out=e[:, cols], in_=v[:, cols], func=ACT.Exp)

        above = keep.tile([P, TILES * J], F32, name="above")
        nc.vector.tensor_scalar(
            out=above[:], in0=v[:], scalar1=-KNEE, scalar2=0.0, op0=ALU.add, op1=ALU.max
        )
        capped = keep.tile([P, TILES * J], F32, name="capped")
        nc.vector.tensor_scalar(
            out=capped[:], in0=e[:], scalar1=math.exp(KNEE), scalar2=None, op0=ALU.min
        )
        rest = keep.tile([P, TILES * J], F32, name="rest")
        for m in range(TILES):
            cols = slice(m * J, (m + 1) * J)
            nc.vector.scalar_tensor_tensor(
                out=rest[:, cols], in0=s_bank[m][:], scalar=-0.5, in1=above[:, cols],
                op0=ALU.mult, op1=ALU.add,
            )
        for m in range(TILES):
            for h in range(2):
                cols = slice(m * J + h * HALF, m * J + (h + 1) * HALF)
                soft = keep.tile([P, HALF], F32, name=f"soft{m}{h}")
                y = keep.tile([P, HALF], F32, name=f"y{m}{h}")
                nc.scalar.activation(out=soft[:], in_=capped[:, cols], func=ACT.Ln, bias=1.0)
                nc.vector.tensor_tensor(out=y[:], in0=soft[:], in1=rest[:, cols], op=ALU.add)
                nc.sync.dma_start(out=out[m * P : (m + 1) * P, h * HALF : (h + 1) * HALF], in_=y[:])
